import numpy as np
import ml_dtypes


def mxq(x, axis, fmt="e4m3"):
    dtype, down = {"e4m3": (ml_dtypes.float8_e4m3fn, 7), "e5m2": (ml_dtypes.float8_e5m2, 14)}[fmt]
    v = np.moveaxis(np.asarray(x, np.float32).astype(ml_dtypes.bfloat16).astype(np.float64), axis, -1)
    blocks = v.reshape(v.shape[:-1] + (-1, 32))
    amax = np.abs(blocks).max(-1, keepdims=True)
    byte = np.maximum(np.where(amax > 0, np.frexp(amax)[1] - 1 + 127, 0) - down, 1)
    scale = np.exp2(byte - 127.0)
    codes = (blocks / scale).astype(np.float32).astype(dtype).astype(np.float64)
    return np.moveaxis((codes * scale).reshape(v.shape), -1, axis)


WIDE = False


def mx_kscale(k):
    if not WIDE:
        return np.ones(k)
    levels = np.array([10, -10, 5, -5, 0])
    if k % 512:
        return np.exp2(np.random.permutation(np.resize(levels, k // 32))).repeat(32)
    a = np.empty((k // 512, 16))
    for p in range(k // 512):
        a[p, :8] = np.random.permutation(np.resize(levels, 8))
        for g in range(8):
            far = levels[np.abs(levels - a[p, g]) >= 10]
            a[p, g + 8] = far[np.random.randint(len(far))]
    return np.exp2(a.ravel()).repeat(32)


def f64(x):
    return np.asarray(x).astype(np.float64)


def striped(idx):
    return np.tile(idx.reshape(-1, 16).T, (8, 1)).astype(np.uint16)


def unstriped(offs):
    return offs[:16].T.reshape(-1).astype(np.int64)


def striped8(idx):
    return np.concatenate([x.reshape(-1, 16).T for x in idx]).astype(np.uint16)


def runs(offs, k):
    lists = np.stack([offs[16 * r : 16 * r + 16].T.reshape(-1) for r in range(8)]).astype(np.int64)
    return lists[np.arange(k) % 512 // 64]


def pack_weight(w):
    k, n = w.shape
    w = f64(np.asarray(w, np.float32).astype(ml_dtypes.bfloat16)).reshape(k // 32, 32, n)
    amax = np.abs(w).max(1)
    byte = np.clip(np.where(amax > 0, np.frexp(amax)[1] - 1 + 127 - 7, 1), 1, 254)
    scaled = (w * np.exp2(127.0 - byte)[:, None, :]).reshape(k, n).astype(np.float32)
    words = np.ascontiguousarray(scaled.reshape(k // 512, 128, 4, n).transpose(0, 1, 3, 2)).astype(ml_dtypes.float8_e4m3fn).view(np.uint8)
    return words, np.ascontiguousarray(byte.astype(np.uint8).reshape(k // 512, 16, n))


def unpack_weight(words, scales):
    g, p, n, _ = words.shape
    vals = np.ascontiguousarray(words).view(ml_dtypes.float8_e4m3fn).astype(np.float64) * np.repeat(np.exp2(scales.astype(np.float64) - 127.0), 8, axis=1)[..., None]
    return vals.transpose(0, 1, 3, 2).reshape(g * 512, n)


E2M1 = np.array([0.0, 0.5, 1.0, 1.5, 2.0, 3.0, 4.0, 6.0, -0.0, -0.5, -1.0, -1.5, -2.0, -3.0, -4.0, -6.0])


def pack_fp4(w):
    k, n = w.shape
    w = f64(np.asarray(w, np.float32).astype(ml_dtypes.bfloat16)).reshape(k // 32, 32, n)
    amax = np.abs(w).max(1)
    mant, ex = np.frexp(amax / 6.0)
    byte = np.clip(np.where(amax > 0, np.where(mant > 0.5, ex, ex - 1) + 127, 1), 1, 254)
    scaled = (w * np.exp2(127.0 - byte)[:, None, :]).reshape(k, n).astype(np.float32)
    c = np.ascontiguousarray(scaled.reshape(k // 512, 128, 4, n).transpose(0, 1, 3, 2)).astype(ml_dtypes.float4_e2m1fn).view(np.uint8) & 0xF
    words = (c[..., 0::2] | (c[..., 1::2] << 4)).reshape(k // 512, 128, 2 * n)
    return np.ascontiguousarray(words), np.ascontiguousarray(byte.astype(np.uint8).reshape(k // 512, 16, n))


def unpack_fp4(words, scales):
    g, _, n = scales.shape
    words = np.ascontiguousarray(words).reshape(g, 128, n, 2)
    nib = np.empty((g, 128, n, 4), np.uint8)
    nib[..., 0::2] = words & 0xF
    nib[..., 1::2] = words >> 4
    vals = E2M1[nib] * np.repeat(np.exp2(scales.astype(np.float64) - 127.0), 8, axis=1)[..., None]
    return vals.transpose(0, 1, 3, 2).reshape(g * 512, n)


def relu(v):
    return np.maximum(v, 0.0)

def planes(y):
    n, m = y.shape
    v = y.astype(np.float32).astype(ml_dtypes.bfloat16).astype(np.float64).reshape(n // 32, 32, m)
    top = np.abs(v).max(1)
    byte = np.clip(np.where(top > 0, np.frexp(top)[1] - 1 + 127 - 7, 1), 1, 254)
    codes = (v * np.exp2(127.0 - byte)[:, None, :]).reshape(n, m).astype(np.float32).astype(ml_dtypes.float8_e4m3fn).view(np.uint8)
    words = codes.reshape(n // 512, 128, 4, m).transpose(0, 1, 3, 2)
    return np.ascontiguousarray(words), np.ascontiguousarray(byte.astype(np.uint8).reshape(n // 512, 16, m))


K, T, S, H, J, G = 512, 2048, 512, 512, 512, 2048


def setup_inputs():
    n = np.random.standard_normal
    s = mx_kscale(K)[:, None]
    packed_xT = pack_weight(n((K, T)) * s)
    packed_w1 = pack_fp4(n((K, H)) / np.sqrt(K) / s)
    packed_dT = pack_weight(n((K, G)) / s)
    return {
        "x_words": packed_xT[0],
        "x_scales": packed_xT[1],
        "w1_words": packed_w1[0],
        "w1_scales": packed_w1[1],
        "tab": n((H, J)).astype(np.float32),
        "gs": (np.random.uniform(0.5, 1.5, (K, 1)) * s).astype(np.float32),
        "d_words": packed_dT[0],
        "d_scales": packed_dT[1],
        "offs": striped(np.random.permutation(T)[:S]),
        "n1": striped8(np.random.randint(0, J, (8, S))),
        "n2": striped8(np.stack([np.random.permutation(S) for _ in range(8)])),
        "k1": striped8(np.random.randint(0, G, (8, H))),
        "n3": striped8(np.stack([np.random.permutation(S) for _ in range(8)])),
        "n4": striped8(np.stack([np.random.permutation(S) for _ in range(8)])),
    }


def reference(x_words, x_scales, w1_words, w1_scales, tab, gs, d_words, d_scales, offs, n1, n2, k1, n3, n4):
    d_k1 = unpack_weight(d_words, d_scales)[np.arange(K)[:, None], runs(k1, K)]
    xq = unpack_weight(x_words, x_scales)[:, unstriped(offs)]
    y = unpack_fp4(w1_words, w1_scales).T @ xq
    z = f64(gs) * (np.abs(y - (y[np.arange(H)[:, None], runs(n2, H)]) - (f64(tab)[np.arange(H)[:, None], runs(n1, H)])))
    h = 0.0625 * ((d_k1.T @ mxq(z, 0, "e4m3")))
    out_0 = relu(h - (h[np.arange(H)[:, None], runs(n3, H)])) + 0.5 * (relu(h[np.arange(H)[:, None], runs(n4, H)] - h))
    return (out_0,) + planes(out_0)

@@ -1,0 +1,247 @@
+from contextlib import ExitStack
+
+import concourse.mybir as mybir
+
+F32 = mybir.dt.float32
+BF16 = mybir.dt.bfloat16
+I32 = mybir.dt.int32
+U32 = mybir.dt.uint32
+U16 = mybir.dt.uint16
+U8 = mybir.dt.uint8
+FP8X4 = mybir.dt.float8_e4m3fn_x4
+FP4X4 = mybir.dt.float4_e2m1fn_x4
+ALU = mybir.AluOpType
+ACT = mybir.ActivationFunctionType
+
+P = 128
+PACK = 4
+ROWS = 512
+S = 512
+TABLE = 2048
+HALF = 256
+HALVES = ((0, HALF), (HALF, HALF))
+Z_CHUNKS = ((0, 256), (256, 256))
+OUT_CHUNKS = ((0, 256), (256, 128), (384, 128))
+
+FLOPS = 2 * 2 * ROWS * ROWS * S
+
+
+def entries(list_tile, start, count):
+    return list_tile[:, start // 16 : (start + count) // 16]
+
+
+def interleaved_views(words, planes):
+    return (
+        words.rearrange("p (c i) t -> p c t i", i=4),
+        planes.rearrange("p t (c i) -> p c t i", i=4),
+    )
+
+
+def tile_picked_densekinddhinge_none_po_kernel(
+    tc, x_words, x_scales, w1_words, w1_scales, tab, gs, d_words, d_scales, offs, n1, n2, k1, n3, n4, out_0, out_1, out_2
+):
+    nc = tc.nc
+    with ExitStack() as ctx:
+        keep = ctx.enter_context(tc.tile_pool(name="keep", bufs=1))
+        psum = ctx.enter_context(tc.psum_pool(name="psum", bufs=8))
+
+        def load_list(name, src):
+            tile = keep.tile([P, S // 16], U16, name=name)
+            nc.sync.dma_start(tile[:], src)
+            return tile
+
+        xs_table = keep.tile([P, TABLE], U8, name="xs_table")
+        ds_table = keep.tile([P, TABLE], U8, name="ds_table")
+        w1s_raw = keep.tile([P, ROWS], U8, name="w1s_raw")
+        d_scale = keep.tile([P, ROWS], U8, name="d_scale", align_bytes=64)
+        nc.vector.memset(xs_table[:, 0 : TABLE // 2].bitcast(I32), 0)
+        nc.gpsimd.memset(xs_table[:, TABLE // 2 : TABLE].bitcast(I32), 0)
+        nc.vector.memset(ds_table[:, 0 : TABLE // 2].bitcast(I32), 0)
+        nc.gpsimd.memset(ds_table[:, TABLE // 2 : TABLE].bitcast(I32), 0)
+        nc.vector.memset(w1s_raw[:].bitcast(I32), 0)
+        nc.gpsimd.memset(d_scale[:].bitcast(I32), 0)
+
+        offs_sb = load_list("offs_sb", offs)
+        w1w_raw = keep.tile([P, 2 * ROWS], U8, name="w1w_raw")
+        nc.sync.dma_start(w1w_raw[:].bitcast(I32), w1_words[0].bitcast(I32))
+        k1_sb = load_list("k1_sb", k1)
+        for q in range(4):
+            nc.sync.dma_start(xs_table[32 * q : 32 * q + 4, :].bitcast(I32), x_scales[0, 4 * q : 4 * q + 4, :].bitcast(I32))
+        nc.sync.dma_start(ds_table[0:P:8, :].bitcast(I32), d_scales[0].bitcast(I32))
+        n1_sb = load_list("n1_sb", n1)
+        n2_sb = load_list("n2_sb", n2)
+        xw_table = keep.tile([P, TABLE], U32, name="xw_table")
+        nc.sync.dma_start(xw_table[:].bitcast(I32), x_words[0].rearrange("p n t -> p (n t)").bitcast(I32))
+        for q in range(4):
+            nc.sync.dma_start(w1s_raw[32 * q : 32 * q + 4, :].bitcast(I32), w1_scales[0, 4 * q : 4 * q + 4, :].bitcast(I32))
+        tab_rows = tab.rearrange("(p t) j -> p t j", t=PACK)
+        tab_sb = []
+        for t in range(PACK):
+            tile = keep.tile([P, S], F32, name=f"tab{t}")
+            nc.sync.dma_start(tile[:], tab_rows[:, t, :])
+            tab_sb.append(tile)
+        gs_sb = keep.tile([P, PACK], F32, name="gs_sb")
+        nc.sync.dma_start(gs_sb[:], gs.rearrange("(p t) o -> p (t o)", t=PACK))
+        dw_table = keep.tile([P, TABLE], U32, name="dw_table")
+        nc.sync.dma_start(dw_table[:].bitcast(I32), d_words[0].rearrange("p n t -> p (n t)").bitcast(I32))
+        n4_sb = load_list("n4_sb", n4)
+        n3_sb = load_list("n3_sb", n3)
+
+        w1_codes = keep.tile([P, PACK, 2 * P], U8, name="w1_codes", align_bytes=64)
+        nc.vector.tensor_copy(
+            w1_codes[:].rearrange("p t (m b) -> p m t b", b=2),
+            w1w_raw[:].rearrange("p (m t b) -> p m t b", t=PACK, b=2),
+        )
+        x_scale = keep.tile([P, S], U8, name="x_scale", align_bytes=64)
+        nc.vector.tensor_copy(x_scale[:], xs_table[:].indirect(offs_sb[:]))
+        ds_picked = keep.tile([P, ROWS], U8, name="ds_picked")
+        nc.vector.tensor_copy(ds_picked[:], ds_table[:].indirect(k1_sb[:]))
+        ds_dealt = keep.tile([P, PACK, P], U8, name="ds_dealt")
+        nc.vector.tensor_copy(ds_dealt[:].rearrange("p t m -> p m t"), ds_picked[:].rearrange("p (m t) -> p m t", t=PACK))
+        w1_scale = keep.tile([P, PACK, P], U8, name="w1_scale", align_bytes=64)
+        nc.vector.tensor_copy(w1_scale[:].rearrange("p t m -> p m t"), w1s_raw[:].rearrange("p (m t) -> p m t", t=PACK))
+        for q in range(4):
+            nc.sync.dma_start(
+                d_scale[32 * q : 32 * q + 4, :].bitcast(I32),
+                ds_dealt[32 * q : 32 * q + 32 : 8, :, :].rearrange("p t m -> p (t m)").bitcast(I32),
+            )
+
+        y = [keep.tile([P, S], F32, name=f"y{t}", tag=f"y{t}", align_bytes=64) for t in range(PACK)]
+        for start, width in HALVES:
+            x_codes = keep.tile([P, width], U32, name=f"x_codes{start}", align_bytes=64)
+            nc.vector.tensor_copy(x_codes[:], xw_table[:].indirect(entries(offs_sb, start, width)))
+            for t in range(PACK):
+                acc = psum.tile([P, width], F32, name="acc")
+                nc.tensor.matmul_mx(
+                    out=acc[:],
+                    lhsT=w1_codes[:, t, :].bitcast(FP4X4),
+                    lhsT_scale=w1_scale[:, t, :],
+                    rhs=x_codes[:].bitcast(FP8X4),
+                    rhs_scale=x_scale[:, start : start + width],
+                    start=True,
+                    stop=True,
+                )
+                nc.scalar.copy(y[t][:, start : start + width], acc[:])
+
+        z_codes = keep.tile([P, S], U32, name="z_codes", align_bytes=64)
+        z_scale = keep.tile([P, S], U8, name="z_scale", align_bytes=64)
+        z_words = []
+        for c, (start, width) in enumerate(Z_CHUNKS):
+            part = []
+            diff = keep.tile([P, PACK, width], F32, name=f"diff{start}")
+            size = keep.tile([P, PACK, width], F32, name=f"size{start}", tag=f"turn{c}")
+            z_planes = keep.tile([P, PACK, width], BF16, name=f"z_planes{start}", tag=f"turn{c + 1}")
+            for step in range(PACK + 1):
+                if step < PACK:
+                    part.append(keep.tile([P, width], F32, name="part", bufs=3))
+                    nc.vector.tensor_tensor(
+                        part[step][:],
+                        tab_sb[step][:].indirect(entries(n1_sb, start, width)),
+                        y[step][:, start : start + width],
+                        ALU.subtract,
+                    )
+                if step > 0:
+                    t = step - 1
+                    nc.vector.tensor_tensor(diff[:, t, :], y[t][:].indirect(entries(n2_sb, start, width)), part[t][:], ALU.add)
+                    nc.scalar.activation(size[:, t, :], diff[:, t, :], ACT.Abs)
+                    nc.scalar.activation(z_planes[:, t, :], size[:, t, :], ACT.Copy, scale=gs_sb[:, t : t + 1])
+            words = keep.tile([P, width, PACK], BF16, name=f"z_words{start}", align_bytes=64)
+            nc.scalar.copy(*interleaved_views(words[:], z_planes[:]))
+            z_words.append(words)
+
+        def quantise_z(c):
+            start, width = Z_CHUNKS[c]
+            nc.vector.quantize_mx(
+                out=z_codes[:, start : start + width].bitcast(FP8X4),
+                scales=z_scale[:, start : start + width],
+                in_=z_words[c][:].rearrange("p j t -> p (j t)"),
+            )
+
+        for c in range(len(Z_CHUNKS) - 1):
+            quantise_z(c)
+        dw_picked = keep.tile([P, ROWS], U32, name="dw_picked", tag="y2", align_bytes=64)
+        nc.vector.tensor_copy(dw_picked[:], dw_table[:].indirect(k1_sb[:]))
+        d_codes = keep.tile([P, PACK, P], U32, name="d_codes", align_bytes=64)
+        dealt = d_codes[:].bitcast(I32).rearrange("p t (c i) -> p c t i", i=4)
+        picked = dw_picked[:].bitcast(I32).rearrange("p (c i t) -> p c t i", i=4, t=PACK)
+        nc.vector.tensor_copy(dealt[:, :, 0, :], picked[:, :, 0, :])
+        quantise_z(len(Z_CHUNKS) - 1)
+        nc.vector.tensor_copy(dealt[:, :, 1:PACK, :], picked[:, :, 1:PACK, :])
+
+        h = [keep.tile([P, S], F32, name=f"h{t}") for t in range(PACK)]
+        h_neg = [keep.tile([P, S], F32, name=f"h_neg{t}") for t in range(PACK)]
+
+        def second_product(t, start, width):
+            acc = psum.tile([P, width], F32, name="acc")
+            nc.tensor.matmul_mx(
+                out=acc[:],
+                lhsT=d_codes[:, t, :].bitcast(FP8X4),
+                lhsT_scale=d_scale[:, t * P : (t + 1) * P],
+                rhs=z_codes[:, start : start + width].bitcast(FP8X4),
+                rhs_scale=z_scale[:, start : start + width],
+                start=True,
+                stop=True,
+            )
+            nc.scalar.activation(h[t][:, start : start + width], acc[:], ACT.Copy, scale=0.0625)
+            nc.scalar.activation(h_neg[t][:, start : start + width], acc[:], ACT.Copy, scale=-0.0625)
+
+        out_rows = out_0.rearrange("(p t) j -> p t j", t=PACK)
+        out_words = out_1[0].rearrange("p n t -> p (n t)").bitcast(I32)
+        result = [keep.tile([P, PACK, width], F32, name=f"result{start}") for start, width in OUT_CHUNKS]
+        half_rise = [keep.tile([P, 2, S], F32, name=f"half_rise{u}") for u in range(2)]
+        out_codes = keep.tile([P, S], U32, name="out_codes", align_bytes=64)
+        out_scale = keep.tile([P, S], U8, name="out_scale", align_bytes=64)
+
+        def fetch_rise(dst, t, start, width):
+            nc.vector.tensor_tensor(dst, h[t][:].indirect(entries(n4_sb, start, width)), h_neg[t][:, start : start + width], ALU.add)
+
+        def fetch_drop(dst, t, start, width):
+            nc.vector.tensor_tensor(dst, h_neg[t][:].indirect(entries(n3_sb, start, width)), h[t][:, start : start + width], ALU.add)
+
+        def combine(u, c, drop_part):
+            start, width = OUT_CHUNKS[c]
+            cols = slice(start, start + width)
+            nc.vector.scalar_tensor_tensor(
+                result[c][:, 2 * u : 2 * u + 2, :], drop_part, 0.0, half_rise[u][:, :, cols], ALU.max, ALU.add
+            )
+            nc.sync.dma_start(out_rows[:, 2 * u : 2 * u + 2, cols], result[c][:, 2 * u : 2 * u + 2, :])
+
+        for start, width in Z_CHUNKS:
+            second_product(0, start, width)
+        second_product(1, 0, S)
+        rise_low = keep.tile([P, 2, S], F32, name="rise_low")
+        drop_low = keep.tile([P, 2, S], F32, name="drop_low")
+        for t in range(2):
+            for start, width in HALVES:
+                fetch_rise(rise_low[:, t, start : start + width], t, start, width)
+            second_product(t + 2, 0, S)
+            nc.scalar.activation(half_rise[0][:, t, :], rise_low[:, t, :], ACT.Relu, scale=0.5)
+            for start, width in HALVES:
+                fetch_drop(drop_low[:, t, start : start + width], t, start, width)
+        for c, (start, width) in enumerate(OUT_CHUNKS):
+            combine(0, c, drop_low[:, :, start : start + width])
+
+        for c, (start, width) in enumerate(OUT_CHUNKS):
+            rise_high = keep.tile([P, 2, width], F32, name=f"rise_high{start}", tag=f"high{c}")
+            for t in (2, 3):
+                fetch_rise(rise_high[:, t - 2, :], t, start, width)
+            nc.scalar.activation(half_rise[1][:, :, start : start + width], rise_high[:], ACT.Relu, scale=0.5)
+
+        for c, (start, width) in enumerate(OUT_CHUNKS):
+            cols = slice(start, start + width)
+            drop_high = keep.tile([P, 2, width], F32, name=f"drop_high{start}", tag=f"high{c}")
+            for t in (2, 3):
+                fetch_drop(drop_high[:, t - 2, :], t, start, width)
+            combine(1, c, drop_high[:])
+            words = keep.tile([P, width, PACK], BF16, name=f"out_words{start}", align_bytes=64)
+            if c < len(OUT_CHUNKS) - 1:
+                nc.scalar.copy(*interleaved_views(words[:], result[c][:]))
+            else:
+                nc.vector.tensor_copy(*interleaved_views(words[:], result[c][:]))
+            nc.vector.quantize_mx(
+                out=out_codes[:, cols].bitcast(FP8X4), scales=out_scale[:, cols], in_=words[:].rearrange("p j t -> p (j t)")
+            )
+            nc.sync.dma_start(out_words[:, cols], out_codes[:, cols].bitcast(I32))
+        for q in range(4):
+            queue = nc.sync if q % 2 == 0 else nc.scalar
+            queue.dma_start(out_2[0, 4 * q : 4 * q + 4, :].bitcast(I32), out_scale[32 * q : 32 * q + 4, :].bitcast(I32))

@@ -15,25 +15,36 @@ ACT = mybir.ActivationFunctionType
 
 P = 128
 PACK = 4
+QUADRANTS = 4
 ROWS = 512
 S = 512
 TABLE = 2048
-HALF = 256
-HALVES = ((0, HALF), (HALF, HALF))
-Z_CHUNKS = ((0, 256), (256, 256))
+LIST_ROWS = 16
+LINE = 16
+PART_BUFS = 3
+H_SCALE = 0.0625
+
+HALVES = ((0, S // 2), (S // 2, S // 2))
 OUT_CHUNKS = ((0, 256), (256, 128), (384, 128))
 
 FLOPS = 2 * 2 * ROWS * ROWS * S
 
 
 def entries(list_tile, start, count):
-    return list_tile[:, start // 16 : (start + count) // 16]
+    return list_tile[:, start // LIST_ROWS : (start + count) // LIST_ROWS]
 
 
 def interleaved_views(words, planes):
     return (
-        words.rearrange("p (c i) t -> p c t i", i=4),
-        planes.rearrange("p t (c i) -> p c t i", i=4),
+        words.rearrange("p (c i) t -> p c t i", i=LINE // 4),
+        planes.rearrange("p t (c i) -> p c t i", i=LINE // 4),
+    )
+
+
+def dealt_byte_views(dealt, plain):
+    return (
+        dealt.rearrange("p t (c i) -> p c t i", i=LINE),
+        plain.rearrange("p (c i t) -> p c t i", i=LINE, t=PACK),
     )
 
 
@@ -46,7 +57,7 @@ def tile_picked_densekinddhinge_none_po_kernel(
         psum = ctx.enter_context(tc.psum_pool(name="psum", bufs=8))
 
         def load_list(name, src):
-            tile = keep.tile([P, S // 16], U16, name=name)
+            tile = keep.tile([P, S // LIST_ROWS], U16, name=name)
             nc.sync.dma_start(tile[:], src)
             return tile
 
@@ -65,14 +76,14 @@ def tile_picked_densekinddhinge_none_po_kernel(
         w1w_raw = keep.tile([P, 2 * ROWS], U8, name="w1w_raw")
         nc.sync.dma_start(w1w_raw[:].bitcast(I32), w1_words[0].bitcast(I32))
         k1_sb = load_list("k1_sb", k1)
-        for q in range(4):
+        for q in range(QUADRANTS):
             nc.sync.dma_start(xs_table[32 * q : 32 * q + 4, :].bitcast(I32), x_scales[0, 4 * q : 4 * q + 4, :].bitcast(I32))
         nc.sync.dma_start(ds_table[0:P:8, :].bitcast(I32), d_scales[0].bitcast(I32))
         n1_sb = load_list("n1_sb", n1)
         n2_sb = load_list("n2_sb", n2)
-        xw_table = keep.tile([P, TABLE], U32, name="xw_table")
+        xw_table = keep.tile([P, TABLE], U32, name="xw_table", tag="xw_table")
         nc.sync.dma_start(xw_table[:].bitcast(I32), x_words[0].rearrange("p n t -> p (n t)").bitcast(I32))
-        for q in range(4):
+        for q in range(QUADRANTS):
             nc.sync.dma_start(w1s_raw[32 * q : 32 * q + 4, :].bitcast(I32), w1_scales[0, 4 * q : 4 * q + 4, :].bitcast(I32))
         tab_rows = tab.rearrange("(p t) j -> p t j", t=PACK)
         tab_sb = []
@@ -89,22 +100,13 @@ def tile_picked_densekinddhinge_none_po_kernel(
 
         w1_codes = keep.tile([P, PACK, 2 * P], U8, name="w1_codes", align_bytes=64)
         nc.vector.tensor_copy(
-            w1_codes[:].rearrange("p t (m b) -> p m t b", b=2),
-            w1w_raw[:].rearrange("p (m t b) -> p m t b", t=PACK, b=2),
+            w1_codes[:].rearrange("p t (c i b) -> p c t i b", i=LINE // 2, b=2),
+            w1w_raw[:].rearrange("p (c i t b) -> p c t i b", i=LINE // 2, t=PACK, b=2),
         )
         x_scale = keep.tile([P, S], U8, name="x_scale", align_bytes=64)
         nc.vector.tensor_copy(x_scale[:], xs_table[:].indirect(offs_sb[:]))
-        ds_picked = keep.tile([P, ROWS], U8, name="ds_picked")
-        nc.vector.tensor_copy(ds_picked[:], ds_table[:].indirect(k1_sb[:]))
-        ds_dealt = keep.tile([P, PACK, P], U8, name="ds_dealt")
-        nc.vector.tensor_copy(ds_dealt[:].rearrange("p t m -> p m t"), ds_picked[:].rearrange("p (m t) -> p m t", t=PACK))
         w1_scale = keep.tile([P, PACK, P], U8, name="w1_scale", align_bytes=64)
-        nc.vector.tensor_copy(w1_scale[:].rearrange("p t m -> p m t"), w1s_raw[:].rearrange("p (m t) -> p m t", t=PACK))
-        for q in range(4):
-            nc.sync.dma_start(
-                d_scale[32 * q : 32 * q + 4, :].bitcast(I32),
-                ds_dealt[32 * q : 32 * q + 32 : 8, :, :].rearrange("p t m -> p (t m)").bitcast(I32),
-            )
+        nc.gpsimd.tensor_copy(*dealt_byte_views(w1_scale[:], w1s_raw[:]))
 
         y = [keep.tile([P, S], F32, name=f"y{t}", tag=f"y{t}", align_bytes=64) for t in range(PACK)]
         for start, width in HALVES:
@@ -123,14 +125,24 @@ def tile_picked_densekinddhinge_none_po_kernel(
                 )
                 nc.scalar.copy(y[t][:, start : start + width], acc[:])
 
+        ds_picked = keep.tile([P, ROWS], U8, name="ds_picked")
+        nc.vector.tensor_copy(ds_picked[:], ds_table[:].indirect(k1_sb[:]))
+        ds_dealt = keep.tile([P, PACK, P], U8, name="ds_dealt", tag="xw_table")
+        nc.vector.tensor_copy(*dealt_byte_views(ds_dealt[:], ds_picked[:]))
+        for q in range(QUADRANTS):
+            nc.sync.dma_start(
+                d_scale[32 * q : 32 * q + 4, :].bitcast(I32),
+                ds_dealt[32 * q : 32 * q + 32 : 8, :, :].rearrange("p t m -> p (t m)").bitcast(I32),
+            )
+
         z_codes = keep.tile([P, S], U32, name="z_codes", align_bytes=64)
         z_scale = keep.tile([P, S], U8, name="z_scale", align_bytes=64)
         z_words = []
-        for c, (start, width) in enumerate(Z_CHUNKS):
+        for c, (start, width) in enumerate(HALVES):
             part = []
             diff = keep.tile([P, PACK, width], F32, name=f"diff{start}")
             size = keep.tile([P, PACK, width], F32, name=f"size{start}", tag=f"turn{c}")
-            z_planes = keep.tile([P, PACK, width], BF16, name=f"z_planes{start}", tag=f"turn{c + 1}")
+            z_pairs = keep.tile([P, 2, width, 2], BF16, name=f"z_pairs{start}", tag=f"turn{c + 1}")
             for step in range(PACK + 1):
                 if step < PACK:
                     part.append(keep.tile([P, width], F32, name="part", bufs=3))
@@ -144,46 +156,52 @@ def tile_picked_densekinddhinge_none_po_kernel(
                     t = step - 1
                     nc.vector.tensor_tensor(diff[:, t, :], y[t][:].indirect(entries(n2_sb, start, width)), part[t][:], ALU.add)
                     nc.scalar.activation(size[:, t, :], diff[:, t, :], ACT.Abs)
-                    nc.scalar.activation(z_planes[:, t, :], size[:, t, :], ACT.Copy, scale=gs_sb[:, t : t + 1])
-            words = keep.tile([P, width, PACK], BF16, name=f"z_words{start}", align_bytes=64)
-            nc.scalar.copy(*interleaved_views(words[:], z_planes[:]))
+                    nc.scalar.activation(z_pairs[:, t // 2, :, t % 2], size[:, t, :], ACT.Copy, scale=gs_sb[:, t : t + 1])
+            words = keep.tile([P, width, PACK], BF16, name=f"z_words{start}", tag=f"z_words{c}", align_bytes=64)
+            nc.scalar.copy(
+                words[:].rearrange("p j t -> p (j t)").bitcast(F32).rearrange("p (j u) -> p j u", u=2),
+                z_pairs[:].rearrange("p u j e -> p u (j e)").bitcast(F32).rearrange("p u j -> p j u"),
+            )
             z_words.append(words)
 
         def quantise_z(c):
-            start, width = Z_CHUNKS[c]
+            start, width = HALVES[c]
             nc.vector.quantize_mx(
                 out=z_codes[:, start : start + width].bitcast(FP8X4),
                 scales=z_scale[:, start : start + width],
                 in_=z_words[c][:].rearrange("p j t -> p (j t)"),
             )
 
-        for c in range(len(Z_CHUNKS) - 1):
-            quantise_z(c)
+        quantise_z(0)
         dw_picked = keep.tile([P, ROWS], U32, name="dw_picked", tag="y2", align_bytes=64)
         nc.vector.tensor_copy(dw_picked[:], dw_table[:].indirect(k1_sb[:]))
-        d_codes = keep.tile([P, PACK, P], U32, name="d_codes", align_bytes=64)
-        dealt = d_codes[:].bitcast(I32).rearrange("p t (c i) -> p c t i", i=4)
-        picked = dw_picked[:].bitcast(I32).rearrange("p (c i t) -> p c t i", i=4, t=PACK)
-        nc.vector.tensor_copy(dealt[:, :, 0, :], picked[:, :, 0, :])
-        quantise_z(len(Z_CHUNKS) - 1)
-        nc.vector.tensor_copy(dealt[:, :, 1:PACK, :], picked[:, :, 1:PACK, :])
+        picked = dw_picked[:].bitcast(I32).rearrange("p (c i t) -> p c t i", i=LINE // 4, t=PACK)
+        d_first = keep.tile([P, P], U32, name="d_first", align_bytes=64)
+        nc.vector.tensor_copy(d_first[:].bitcast(I32).rearrange("p (c i) -> p c i", i=LINE // 4), picked[:, :, 0, :])
+        quantise_z(1)
+        d_rest = keep.tile([P, PACK - 1, P], U32, name="d_rest", tag="z_words1", align_bytes=64)
+        nc.vector.tensor_copy(d_rest[:].bitcast(I32).rearrange("p t (c i) -> p c t i", i=LINE // 4), picked[:, :, 1:PACK, :])
+        d_codes = [d_first[:]] + [d_rest[:, t, :] for t in range(PACK - 1)]
 
-        h = [keep.tile([P, S], F32, name=f"h{t}") for t in range(PACK)]
+        h = [keep.tile([P, S], F32, name=f"h{t}", tag="turn2" if t == 0 else f"h{t}") for t in range(PACK)]
         h_neg = [keep.tile([P, S], F32, name=f"h_neg{t}") for t in range(PACK)]
 
         def second_product(t, start, width):
             acc = psum.tile([P, width], F32, name="acc")
             nc.tensor.matmul_mx(
                 out=acc[:],
-                lhsT=d_codes[:, t, :].bitcast(FP8X4),
+                lhsT=d_codes[t].bitcast(FP8X4),
                 lhsT_scale=d_scale[:, t * P : (t + 1) * P],
                 rhs=z_codes[:, start : start + width].bitcast(FP8X4),
                 rhs_scale=z_scale[:, start : start + width],
                 start=True,
                 stop=True,
             )
-            nc.scalar.activation(h[t][:, start : start + width], acc[:], ACT.Copy, scale=0.0625)
-            nc.scalar.activation(h_neg[t][:, start : start + width], acc[:], ACT.Copy, scale=-0.0625)
+            nc.scalar.activation(h[t][:, start : start + width], acc[:], ACT.Copy, scale=H_SCALE)
+            if (t, start) == (0, 0):
+                nc.vector.tensor_scalar_mul(h_neg[t][:, 0:width], h[t][:, 0:width], -1.0)
+            else:
+                nc.scalar.activation(h_neg[t][:, start : start + width], acc[:], ACT.Copy, scale=-H_SCALE)
 
         out_rows = out_0.rearrange("(p t) j -> p t j", t=PACK)
         out_words = out_1[0].rearrange("p n t -> p (n t)").bitcast(I32)
@@ -206,7 +224,7 @@ def tile_picked_densekinddhinge_none_po_kernel(
             )
             nc.sync.dma_start(out_rows[:, 2 * u : 2 * u + 2, cols], result[c][:, 2 * u : 2 * u + 2, :])
 
-        for start, width in Z_CHUNKS:
+        for start, width in HALVES:
             second_product(0, start, width)
         second_product(1, 0, S)
         rise_low = keep.tile([P, 2, S], F32, name="rise_low")
@@ -221,7 +239,7 @@ def tile_picked_densekinddhinge_none_po_kernel(
         for c, (start, width) in enumerate(OUT_CHUNKS):
             combine(0, c, drop_low[:, :, start : start + width])
 
-        for c, (start, width) in enumerate(OUT_CHUNKS):
+        for c, (start, width) in enumerate(HALVES):
             rise_high = keep.tile([P, 2, width], F32, name=f"rise_high{start}", tag=f"high{c}")
             for t in (2, 3):
                 fetch_rise(rise_high[:, t - 2, :], t, start, width)
@@ -229,19 +247,19 @@ def tile_picked_densekinddhinge_none_po_kernel(
 
         for c, (start, width) in enumerate(OUT_CHUNKS):
             cols = slice(start, start + width)
-            drop_high = keep.tile([P, 2, width], F32, name=f"drop_high{start}", tag=f"high{c}")
+            drop_high = keep.tile([P, 2, width], F32, name=f"drop_high{start}", tag=f"high{c % 2}")
             for t in (2, 3):
                 fetch_drop(drop_high[:, t - 2, :], t, start, width)
             combine(1, c, drop_high[:])
-            words = keep.tile([P, width, PACK], BF16, name=f"out_words{start}", align_bytes=64)
+            rounded = keep.tile([P, width, PACK], BF16, name=f"out_words{start}", align_bytes=64)
             if c < len(OUT_CHUNKS) - 1:
-                nc.scalar.copy(*interleaved_views(words[:], result[c][:]))
+                nc.scalar.copy(*interleaved_views(rounded[:], result[c][:]))
             else:
-                nc.vector.tensor_copy(*interleaved_views(words[:], result[c][:]))
+                nc.vector.tensor_copy(*interleaved_views(rounded[:], result[c][:]))
             nc.vector.quantize_mx(
-                out=out_codes[:, cols].bitcast(FP8X4), scales=out_scale[:, cols], in_=words[:].rearrange("p j t -> p (j t)")
+                out=out_codes[:, cols].bitcast(FP8X4), scales=out_scale[:, cols], in_=rounded[:].rearrange("p j t -> p (j t)")
             )
             nc.sync.dma_start(out_words[:, cols], out_codes[:, cols].bitcast(I32))
-        for q in range(4):
+        for q in range(QUADRANTS):
             queue = nc.sync if q % 2 == 0 else nc.scalar
             queue.dma_start(out_2[0, 4 * q : 4 * q + 4, :].bitcast(I32), out_scale[32 * q : 32 * q + 4, :].bitcast(I32))

from contextlib import ExitStack

import concourse.mybir as mybir

F32 = mybir.dt.float32
BF16 = mybir.dt.bfloat16
I32 = mybir.dt.int32
U32 = mybir.dt.uint32
U16 = mybir.dt.uint16
U8 = mybir.dt.uint8
FP8X4 = mybir.dt.float8_e4m3fn_x4
FP4X4 = mybir.dt.float4_e2m1fn_x4
ALU = mybir.AluOpType
ACT = mybir.ActivationFunctionType

P = 128
PACK = 4
QUADRANTS = 4
ROWS = 512
S = 512
TABLE = 2048
LIST_ROWS = 16
LINE = 16
PART_BUFS = 3
H_SCALE = 0.0625

HALVES = ((0, S // 2), (S // 2, S // 2))
OUT_CHUNKS = ((0, 256), (256, 128), (384, 128))

FLOPS = 2 * 2 * ROWS * ROWS * S


def entries(list_tile, start, count):
    return list_tile[:, start // LIST_ROWS : (start + count) // LIST_ROWS]


def interleaved_views(words, planes):
    return (
        words.rearrange("p (c i) t -> p c t i", i=LINE // 4),
        planes.rearrange("p t (c i) -> p c t i", i=LINE // 4),
    )


def dealt_byte_views(dealt, plain):
    return (
        dealt.rearrange("p t (c i) -> p c t i", i=LINE),
        plain.rearrange("p (c i t) -> p c t i", i=LINE, t=PACK),
    )


def tile_picked_densekinddhinge_none_po_kernel(
    tc, x_words, x_scales, w1_words, w1_scales, tab, gs, d_words, d_scales, offs, n1, n2, k1, n3, n4, out_0, out_1, out_2
):
    nc = tc.nc
    with ExitStack() as ctx:
        keep = ctx.enter_context(tc.tile_pool(name="keep", bufs=1))
        psum = ctx.enter_context(tc.psum_pool(name="psum", bufs=8))

        def load_list(name, src):
            tile = keep.tile([P, S // LIST_ROWS], U16, name=name)
            nc.sync.dma_start(tile[:], src)
            return tile

        xs_table = keep.tile([P, TABLE], U8, name="xs_table")
        ds_table = keep.tile([P, TABLE], U8, name="ds_table")
        w1s_raw = keep.tile([P, ROWS], U8, name="w1s_raw")
        d_scale = keep.tile([P, ROWS], U8, name="d_scale", align_bytes=64)
        nc.vector.memset(xs_table[:, 0 : TABLE // 2].bitcast(I32), 0)
        nc.gpsimd.memset(xs_table[:, TABLE // 2 : TABLE].bitcast(I32), 0)
        nc.vector.memset(ds_table[:, 0 : TABLE // 2].bitcast(I32), 0)
        nc.gpsimd.memset(ds_table[:, TABLE // 2 : TABLE].bitcast(I32), 0)
        nc.vector.memset(w1s_raw[:].bitcast(I32), 0)
        nc.gpsimd.memset(d_scale[:].bitcast(I32), 0)

        offs_sb = load_list("offs_sb", offs)
        w1w_raw = keep.tile([P, 2 * ROWS], U8, name="w1w_raw")
        nc.sync.dma_start(w1w_raw[:].bitcast(I32), w1_words[0].bitcast(I32))
        k1_sb = load_list("k1_sb", k1)
        for q in range(QUADRANTS):
            nc.sync.dma_start(xs_table[32 * q : 32 * q + 4, :].bitcast(I32), x_scales[0, 4 * q : 4 * q + 4, :].bitcast(I32))
        nc.sync.dma_start(ds_table[0:P:8, :].bitcast(I32), d_scales[0].bitcast(I32))
        n1_sb = load_list("n1_sb", n1)
        n2_sb = load_list("n2_sb", n2)
        xw_table = keep.tile([P, TABLE], U32, name="xw_table", tag="xw_table")
        nc.sync.dma_start(xw_table[:].bitcast(I32), x_words[0].rearrange("p n t -> p (n t)").bitcast(I32))
        for q in range(QUADRANTS):
            nc.sync.dma_start(w1s_raw[32 * q : 32 * q + 4, :].bitcast(I32), w1_scales[0, 4 * q : 4 * q + 4, :].bitcast(I32))
        tab_rows = tab.rearrange("(p t) j -> p t j", t=PACK)
        tab_sb = []
        for t in range(PACK):
            tile = keep.tile([P, S], F32, name=f"tab{t}")
            nc.sync.dma_start(tile[:], tab_rows[:, t, :])
            tab_sb.append(tile)
        gs_sb = keep.tile([P, PACK], F32, name="gs_sb")
        nc.sync.dma_start(gs_sb[:], gs.rearrange("(p t) o -> p (t o)", t=PACK))
        dw_table = keep.tile([P, TABLE], U32, name="dw_table")
        nc.sync.dma_start(dw_table[:].bitcast(I32), d_words[0].rearrange("p n t -> p (n t)").bitcast(I32))
        n4_sb = load_list("n4_sb", n4)
        n3_sb = load_list("n3_sb", n3)

        w1_codes = keep.tile([P, PACK, 2 * P], U8, name="w1_codes", align_bytes=64)
        nc.vector.tensor_copy(
            w1_codes[:].rearrange("p t (c i b) -> p c t i b", i=LINE // 2, b=2),
            w1w_raw[:].rearrange("p (c i t b) -> p c t i b", i=LINE // 2, t=PACK, b=2),
        )
        x_scale = keep.tile([P, S], U8, name="x_scale", align_bytes=64)
        nc.vector.tensor_copy(x_scale[:], xs_table[:].indirect(offs_sb[:]))
        w1_scale = keep.tile([P, PACK, P], U8, name="w1_scale", align_bytes=64)
        nc.gpsimd.tensor_copy(*dealt_byte_views(w1_scale[:], w1s_raw[:]))

        y = [keep.tile([P, S], F32, name=f"y{t}", tag=f"y{t}", align_bytes=64) for t in range(PACK)]
        for start, width in HALVES:
            x_codes = keep.tile([P, width], U32, name=f"x_codes{start}", align_bytes=64)
            nc.vector.tensor_copy(x_codes[:], xw_table[:].indirect(entries(offs_sb, start, width)))
            for t in range(PACK):
                acc = psum.tile([P, width], F32, name="acc")
                nc.tensor.matmul_mx(
                    out=acc[:],
                    lhsT=w1_codes[:, t, :].bitcast(FP4X4),
                    lhsT_scale=w1_scale[:, t, :],
                    rhs=x_codes[:].bitcast(FP8X4),
                    rhs_scale=x_scale[:, start : start + width],
                    start=True,
                    stop=True,
                )
                nc.scalar.copy(y[t][:, start : start + width], acc[:])

        ds_picked = keep.tile([P, ROWS], U8, name="ds_picked")
        nc.vector.tensor_copy(ds_picked[:], ds_table[:].indirect(k1_sb[:]))
        ds_dealt = keep.tile([P, PACK, P], U8, name="ds_dealt", tag="xw_table")
        nc.vector.tensor_copy(*dealt_byte_views(ds_dealt[:], ds_picked[:]))
        for q in range(QUADRANTS):
            nc.sync.dma_start(
                d_scale[32 * q : 32 * q + 4, :].bitcast(I32),
                ds_dealt[32 * q : 32 * q + 32 : 8, :, :].rearrange("p t m -> p (t m)").bitcast(I32),
            )

        z_codes = keep.tile([P, S], U32, name="z_codes", align_bytes=64)
        z_scale = keep.tile([P, S], U8, name="z_scale", align_bytes=64)
        z_words = []
        for c, (start, width) in enumerate(HALVES):
            part = []
            diff = keep.tile([P, PACK, width], F32, name=f"diff{start}")
            size = keep.tile([P, PACK, width], F32, name=f"size{start}", tag=f"turn{c}")
            z_pairs = keep.tile([P, 2, width, 2], BF16, name=f"z_pairs{start}", tag=f"turn{c + 1}")
            for step in range(PACK + 1):
                if step < PACK:
                    part.append(keep.tile([P, width], F32, name="part", bufs=3))
                    nc.vector.tensor_tensor(
                        part[step][:],
                        tab_sb[step][:].indirect(entries(n1_sb, start, width)),
                        y[step][:, start : start + width],
                        ALU.subtract,
                    )
                if step > 0:
                    t = step - 1
                    nc.vector.tensor_tensor(diff[:, t, :], y[t][:].indirect(entries(n2_sb, start, width)), part[t][:], ALU.add)
                    nc.scalar.activation(size[:, t, :], diff[:, t, :], ACT.Abs)
                    nc.scalar.activation(z_pairs[:, t // 2, :, t % 2], size[:, t, :], ACT.Copy, scale=gs_sb[:, t : t + 1])
            words = keep.tile([P, width, PACK], BF16, name=f"z_words{start}", tag=f"z_words{c}", align_bytes=64)
            nc.scalar.copy(
                words[:].rearrange("p j t -> p (j t)").bitcast(F32).rearrange("p (j u) -> p j u", u=2),
                z_pairs[:].rearrange("p u j e -> p u (j e)").bitcast(F32).rearrange("p u j -> p j u"),
            )
            z_words.append(words)

        def quantise_z(c):
            start, width = HALVES[c]
            nc.vector.quantize_mx(
                out=z_codes[:, start : start + width].bitcast(FP8X4),
                scales=z_scale[:, start : start + width],
                in_=z_words[c][:].rearrange("p j t -> p (j t)"),
            )

        quantise_z(0)
        dw_picked = keep.tile([P, ROWS], U32, name="dw_picked", tag="y2", align_bytes=64)
        nc.vector.tensor_copy(dw_picked[:], dw_table[:].indirect(k1_sb[:]))
        picked = dw_picked[:].bitcast(I32).rearrange("p (c i t) -> p c t i", i=LINE // 4, t=PACK)
        d_first = keep.tile([P, P], U32, name="d_first", align_bytes=64)
        nc.vector.tensor_copy(d_first[:].bitcast(I32).rearrange("p (c i) -> p c i", i=LINE // 4), picked[:, :, 0, :])
        quantise_z(1)
        d_rest = keep.tile([P, PACK - 1, P], U32, name="d_rest", tag="z_words1", align_bytes=64)
        nc.vector.tensor_copy(d_rest[:].bitcast(I32).rearrange("p t (c i) -> p c t i", i=LINE // 4), picked[:, :, 1:PACK, :])
        d_codes = [d_first[:]] + [d_rest[:, t, :] for t in range(PACK - 1)]

        h = [keep.tile([P, S], F32, name=f"h{t}", tag="turn2" if t == 0 else f"h{t}") for t in range(PACK)]
        h_neg = [keep.tile([P, S], F32, name=f"h_neg{t}") for t in range(PACK)]

        def second_product(t, start, width):
            acc = psum.tile([P, width], F32, name="acc")
            nc.tensor.matmul_mx(
                out=acc[:],
                lhsT=d_codes[t].bitcast(FP8X4),
                lhsT_scale=d_scale[:, t * P : (t + 1) * P],
                rhs=z_codes[:, start : start + width].bitcast(FP8X4),
                rhs_scale=z_scale[:, start : start + width],
                start=True,
                stop=True,
            )
            nc.scalar.activation(h[t][:, start : start + width], acc[:], ACT.Copy, scale=H_SCALE)
            if (t, start) == (0, 0):
                nc.vector.tensor_scalar_mul(h_neg[t][:, 0:width], h[t][:, 0:width], -1.0)
            else:
                nc.scalar.activation(h_neg[t][:, start : start + width], acc[:], ACT.Copy, scale=-H_SCALE)

        out_rows = out_0.rearrange("(p t) j -> p t j", t=PACK)
        out_words = out_1[0].rearrange("p n t -> p (n t)").bitcast(I32)
        result = [keep.tile([P, PACK, width], F32, name=f"result{start}") for start, width in OUT_CHUNKS]
        half_rise = [keep.tile([P, 2, S], F32, name=f"half_rise{u}") for u in range(2)]
        out_codes = keep.tile([P, S], U32, name="out_codes", align_bytes=64)
        out_scale = keep.tile([P, S], U8, name="out_scale", align_bytes=64)

        def fetch_rise(dst, t, start, width):
            nc.vector.tensor_tensor(dst, h[t][:].indirect(entries(n4_sb, start, width)), h_neg[t][:, start : start + width], ALU.add)

        def fetch_drop(dst, t, start, width):
            nc.vector.tensor_tensor(dst, h_neg[t][:].indirect(entries(n3_sb, start, width)), h[t][:, start : start + width], ALU.add)

        def combine(u, c, drop_part):
            start, width = OUT_CHUNKS[c]
            cols = slice(start, start + width)
            nc.vector.scalar_tensor_tensor(
                result[c][:, 2 * u : 2 * u + 2, :], drop_part, 0.0, half_rise[u][:, :, cols], ALU.max, ALU.add
            )
            nc.sync.dma_start(out_rows[:, 2 * u : 2 * u + 2, cols], result[c][:, 2 * u : 2 * u + 2, :])

        for start, width in HALVES:
            second_product(0, start, width)
        second_product(1, 0, S)
        rise_low = keep.tile([P, 2, S], F32, name="rise_low")
        drop_low = keep.tile([P, 2, S], F32, name="drop_low")
        for t in range(2):
            for start, width in HALVES:
                fetch_rise(rise_low[:, t, start : start + width], t, start, width)
            second_product(t + 2, 0, S)
            nc.scalar.activation(half_rise[0][:, t, :], rise_low[:, t, :], ACT.Relu, scale=0.5)
            for start, width in HALVES:
                fetch_drop(drop_low[:, t, start : start + width], t, start, width)
        for c, (start, width) in enumerate(OUT_CHUNKS):
            combine(0, c, drop_low[:, :, start : start + width])

        for c, (start, width) in enumerate(HALVES):
            rise_high = keep.tile([P, 2, width], F32, name=f"rise_high{start}", tag=f"high{c}")
            for t in (2, 3):
                fetch_rise(rise_high[:, t - 2, :], t, start, width)
            nc.scalar.activation(half_rise[1][:, :, start : start + width], rise_high[:], ACT.Relu, scale=0.5)

        for c, (start, width) in enumerate(OUT_CHUNKS):
            cols = slice(start, start + width)
            drop_high = keep.tile([P, 2, width], F32, name=f"drop_high{start}", tag=f"high{c % 2}")
            for t in (2, 3):
                fetch_drop(drop_high[:, t - 2, :], t, start, width)
            combine(1, c, drop_high[:])
            rounded = keep.tile([P, width, PACK], BF16, name=f"out_words{start}", align_bytes=64)
            if c < len(OUT_CHUNKS) - 1:
                nc.scalar.copy(*interleaved_views(rounded[:], result[c][:]))
            else:
                nc.vector.tensor_copy(*interleaved_views(rounded[:], result[c][:]))
            nc.vector.quantize_mx(
                out=out_codes[:, cols].bitcast(FP8X4), scales=out_scale[:, cols], in_=rounded[:].rearrange("p j t -> p (j t)")
            )
            nc.sync.dma_start(out_words[:, cols], out_codes[:, cols].bitcast(I32))
        for q in range(QUADRANTS):
            queue = nc.sync if q % 2 == 0 else nc.scalar
            queue.dma_start(out_2[0, 4 * q : 4 * q + 4, :].bitcast(I32), out_scale[32 * q : 32 * q + 4, :].bitcast(I32))
